import numpy as np
import ml_dtypes


def mxq(x, axis, fmt="e4m3"):
    dtype, down = {"e4m3": (ml_dtypes.float8_e4m3fn, 7), "e5m2": (ml_dtypes.float8_e5m2, 14)}[fmt]
    v = np.moveaxis(np.asarray(x, np.float32).astype(ml_dtypes.bfloat16).astype(np.float64), axis, -1)
    blocks = v.reshape(v.shape[:-1] + (-1, 32))
    amax = np.abs(blocks).max(-1, keepdims=True)
    byte = np.maximum(np.where(amax > 0, np.frexp(amax)[1] - 1 + 127, 0) - down, 1)
    scale = np.exp2(byte - 127.0)
    codes = (blocks / scale).astype(np.float32).astype(dtype).astype(np.float64)
    return np.moveaxis((codes * scale).reshape(v.shape), -1, axis)


WIDE = False


def mx_kscale(k):
    if not WIDE:
        return np.ones(k)
    levels = np.array([10, -10, 5, -5, 0])
    if k % 512:
        return np.exp2(np.random.permutation(np.resize(levels, k // 32))).repeat(32)
    a = np.empty((k // 512, 16))
    for p in range(k // 512):
        a[p, :8] = np.random.permutation(np.resize(levels, 8))
        for g in range(8):
            far = levels[np.abs(levels - a[p, g]) >= 10]
            a[p, g + 8] = far[np.random.randint(len(far))]
    return np.exp2(a.ravel()).repeat(32)


BF16 = ml_dtypes.bfloat16


def bf(x):
    return np.asarray(x, np.float32).astype(BF16)


def f64(x):
    return np.asarray(x).astype(np.float64)


E2M1 = np.array([0.0, 0.5, 1.0, 1.5, 2.0, 3.0, 4.0, 6.0, -0.0, -0.5, -1.0, -1.5, -2.0, -3.0, -4.0, -6.0])


def pack_weight(w, fmt):
    k, n = w.shape
    w = f64(bf(w)).reshape(k // 32, 32, n)
    amax = np.abs(w).max(1)
    if fmt == "e4m3":
        byte = np.frexp(amax)[1] - 1 + 127 - 7
    else:
        mant, ex = np.frexp(amax / 6.0)
        byte = np.where(mant > 0.5, ex, ex - 1) + 127
    byte = np.clip(np.where(amax > 0, byte, 1), 1, 254)
    scaled = (w * np.exp2(127.0 - byte)[:, None, :]).reshape(k, n).astype(np.float32)
    by_word = np.ascontiguousarray(scaled.reshape(k // 512, 128, 4, n).transpose(0, 1, 3, 2))
    if fmt == "e4m3":
        words = by_word.astype(ml_dtypes.float8_e4m3fn).view(np.uint8)
    else:
        c = by_word.astype(ml_dtypes.float4_e2m1fn).view(np.uint8) & 0xF
        words = c[..., 0::2] | (c[..., 1::2] << 4)
    return np.ascontiguousarray(words), np.ascontiguousarray(byte.astype(np.uint8).reshape(k // 512, 16, n))


def unpack_weight(words, scales, fmt):
    g, p, n, _ = words.shape
    if fmt == "e4m3":
        vals = np.ascontiguousarray(words).view(ml_dtypes.float8_e4m3fn).astype(np.float64)
    else:
        nib = np.empty((g, p, n, 4), np.uint8)
        nib[..., 0::2] = words & 0xF
        nib[..., 1::2] = words >> 4
        vals = E2M1[nib]
    vals = vals * np.repeat(np.exp2(scales.astype(np.float64) - 127.0), 8, axis=1)[..., None]
    return vals.transpose(0, 1, 3, 2).reshape(g * 512, n)
def pack4(w):
    words, scales = pack_weight(w, "e2m1")
    return words.reshape(words.shape[0], 128, -1), scales


def unpack4(words, scales):
    return unpack_weight(words.reshape(words.shape[0], 128, -1, 2), scales, "e2m1")


B, D, H = 512, 1024, 1536


def draw0():
    s = mx_kscale(D)
    t = mx_kscale(H)
    u = np.random.standard_normal((H, H)) / np.sqrt(H) / t[:, None]
    u_words, u_scales = pack4(u)
    return {
        "x1": bf(np.random.standard_normal((B, D)) * s),
        "x2": bf(np.random.standard_normal((B, D)) * s),
        "h0": bf(np.tanh(np.random.standard_normal((B, H)))),
        "gain": bf((1 + 0.1 * np.random.standard_normal(H)) * t),
        "w": bf(np.random.standard_normal((D, H)) / np.sqrt(D) / s[:, None]),
        "u_words": u_words,
        "u_scales": u_scales,
    }


def core(x1, x2, h0, gain, w, u_words, u_scales):
    wq = mxq(f64(w), 0, "e4m3")
    u = unpack4(u_words, u_scales)
    c = f64(gain)
    r0 = mxq(f64(h0) * c, 1, "e4m3")
    h1 = np.tanh((mxq(f64(x1), 1, "e4m3") @ wq) + (r0 @ u))
    r1 = mxq(h1 * c, 1, "e4m3")
    h2 = np.tanh((mxq(f64(x2), 1, "e4m3") @ wq) + (r1 @ u))
    return h1, h2


def e4m3fn_bytes(y):
    return np.clip(np.asarray(y, np.float64), -448.0, 448.0).astype(np.float32).astype(ml_dtypes.float8_e4m3fn).view(np.uint8)


def e4m3fn_values(b):
    return np.asarray(b, np.uint8).view(ml_dtypes.float8_e4m3fn).astype(np.float64)


def setup_inputs():
    d = draw0()
    x0 = np.asarray(d['w']).astype(np.float64)
    s = (np.max(np.abs(x0), axis=(1,), keepdims=True) / 448.0).astype(np.float32)
    out = {}
    for k, v in d.items():
        if k == 'w':
            out['w_bytes'] = e4m3fn_bytes(x0 / s.astype(np.float64))
            out['w_scale'] = s
        else:
            out[k] = v
    return out


def reference(x1, x2, h0, gain, w_bytes, w_scale, u_words, u_scales):
    return core(x1, x2, h0, gain, e4m3fn_values(w_bytes) * w_scale.astype(np.float64), u_words, u_scales)

@@ -1,0 +1,389 @@
+from contextlib import ExitStack
+
+import concourse.mybir as mybir
+from concourse.masks import make_identity
+
+B, D, H = 512, 1024, 1536
+FLOPS = 2 * 2 * B * H * (D + H)
+
+F32 = mybir.dt.float32
+BF16 = mybir.dt.bfloat16
+I32 = mybir.dt.int32
+U32 = mybir.dt.uint32
+U8 = mybir.dt.uint8
+E4M3 = mybir.dt.float8_e4m3fn
+E4M3X4 = mybir.dt.float8_e4m3fn_x4
+E2M1X4 = mybir.dt.float4_e2m1fn_x4
+MULT = mybir.AluOpType.mult
+COPY = mybir.ActivationFunctionType.Copy
+TANH = mybir.ActivationFunctionType.Tanh
+
+P = 128
+N = 512
+NB = B // P
+NJ = H // N
+NX = D // N
+
+
+def tile_two_step_rnn_fp4_s3_kernel(tc, x1, x2, h0, gain, w_bytes, w_scale, u_words, u_scales, out_0, out_1):
+    nc = tc.nc
+    with ExitStack() as ctx:
+        keep = ctx.enter_context(tc.tile_pool(name="keep", bufs=1))
+        work = ctx.enter_context(tc.tile_pool(name="work", bufs=3))
+        outs = ctx.enter_context(tc.tile_pool(name="outs", bufs=12))
+        psum = ctx.enter_context(tc.psum_pool(name="psum", bufs=1))
+        ctx.enter_context(tc.manual_schedule())
+
+        def keep_tile(shape, dtype, name):
+            return keep.tile(shape, dtype, name=name, align_bytes=64)
+
+        warm = keep_tile([P, 16], F32, "warm")
+        nc.vector.memset(warm[:], 0.0)
+        nc.scalar.activation(out=warm[:, 0:1], in_=warm[:, 8:9], func=TANH)
+        ident = keep_tile([P, P], F32, "ident")
+        make_identity(nc, ident[:])
+        u_planes = keep_tile([P, NJ, H], U8, "u_planes")
+        nc.vector.memset(u_planes[:].rearrange("p g n -> p (g n)").bitcast(I32), 0)
+
+        gain_col = keep_tile([P, NJ, 4], BF16, "gain_col")
+        nc.scalar.dma_start(out=gain_col[:], in_=gain.rearrange("(g p t) -> p g t", p=P, t=4))
+        w_sc = keep_tile([P, NX, 4], F32, "w_sc")
+        nc.scalar.dma_start(out=w_sc[:], in_=w_scale.rearrange("(g p t) o -> p g (t o)", p=P, t=4))
+
+        h0_raw = {}
+        u_sb = {}
+        w_raw = {}
+        x_raw = {}
+
+        def load_h0(g):
+            for pair in range(2):
+                t = keep_tile([P, 2, N], BF16, "h0_%d_%d" % (g, pair))
+                nc.sync.dma_start(
+                    out=t[:],
+                    in_=h0[256 * pair : 256 * pair + 256, N * g : N * g + N].rearrange("(b p) k -> p b k", p=P),
+                )
+                h0_raw[g, pair] = t
+
+        def load_u(g):
+            t = keep_tile([P, 2 * H], U8, "u_%d" % g)
+            nc.sync.dma_start(out=t[:].bitcast(I32), in_=u_words[g].bitcast(I32))
+            u_sb[g] = t
+
+        def load_u_scales():
+            for q in range(4):
+                nc.sync.dma_start(
+                    out=u_planes[32 * q : 32 * q + 4, :, :].bitcast(I32),
+                    in_=u_scales[:, 4 * q : 4 * q + 4, :].rearrange("g q n -> q g n").bitcast(I32),
+                )
+
+        def load_w(g, j0, j1):
+            t = keep_tile([P, 4, N * (j1 - j0)], U8, "w_bytes_%d_%d" % (g, j0))
+            nc.sync.dma_start(
+                out=t[:],
+                in_=w_bytes[N * g : N * g + N, N * j0 : N * j1].rearrange("(p t) n -> p t n", t=4),
+            )
+            for j in range(j0, j1):
+                w_raw[j, g] = (t, N * (j - j0))
+
+        def load_x(s, x):
+            for b in range(NB):
+                t = keep_tile([P, D], BF16, "x%d_%d" % (s, b))
+                nc.sync.dma_start(out=t[:], in_=x[P * b : P * b + P, :])
+                x_raw[s, b] = t
+
+        load_h0(0)
+        load_u(0)
+        load_u_scales()
+        load_w(0, 0, 1)
+        load_h0(1)
+        load_u(1)
+        load_h0(2)
+        load_u(2)
+        load_w(1, 0, 1)
+        load_x(1, x1)
+        load_x(2, x2)
+        load_w(0, 1, 3)
+        load_w(1, 1, 3)
+        gain_row = keep_tile([P, H], BF16, "gain_row")
+        nc.sync.dma_start(out=gain_row[:], in_=gain.partition_broadcast(P))
+
+        r_grp, r_codes, r_scales = {}, {}, {}
+        for s in (1, 2):
+            for g in range(NJ):
+                for pair in range(2):
+                    key = "%d_%d_%d" % (s, g, pair)
+                    r_grp[s, g, pair] = keep_tile([P, 1024], BF16, "rg_" + key)
+                    r_codes[s, g, pair] = keep_tile([P, 256], U32, "rc_" + key)
+                    r_scales[s, g, pair] = keep_tile([P, 256], U8, "rs_" + key)
+        x_grp, x_codes, x_scales = {}, {}, {}
+        for s in (1, 2):
+            for b in range(NB):
+                key = "%d_%d" % (s, b)
+                x_grp[s, b] = keep_tile([P, 1024], BF16, "xg_" + key)
+                x_codes[s, b] = keep_tile([P, 256], U32, "xc_" + key)
+                x_scales[s, b] = keep_tile([P, 256], U8, "xs_" + key)
+        w_codes = {}
+        w_planes = {}
+        for j in range(NJ):
+            for g in range(NX):
+                w_codes[j, g] = keep_tile([P, N], U32, "wc_%d_%d" % (j, g))
+                w_planes[j, g] = keep_tile([P, N], U8, "wp_%d_%d" % (j, g))
+
+        def turn_bank(i):
+            return psum.tile([P, N], F32, tag="turn%d" % i, name="turn%d" % i)
+
+        def h0_turn(g, pair):
+            bank = turn_bank(pair)
+            words = h0_raw[g, pair][:].rearrange("p b k -> p (b k)").bitcast(F32)
+            for u in range(2):
+                for b in range(2):
+                    nc.tensor.transpose(
+                        bank[:, 256 * u + P * b : 256 * u + P * b + P],
+                        words[:, 256 * b + u : 256 * b + 256 : 2],
+                        ident[:],
+                    )
+            nc.vector.tensor_tensor(
+                out=r_grp[1, g, pair][:].rearrange("p (b u e) -> p b u e", u=2, e=2),
+                in0=bank[:].bitcast(BF16).rearrange("p (u b e) -> p b u e", u=2, e=2),
+                in1=gain_col[:, g, :].rearrange("p (u e) -> p u e", e=2).unsqueeze(1).to_broadcast([P, 256, 2, 2]),
+                op=MULT,
+            )
+
+        def r_quant(s, g, pair):
+            nc.vector.quantize_mx(
+                out=r_codes[s, g, pair][:].bitcast(E4M3X4), scales=r_scales[s, g, pair][:], in_=r_grp[s, g, pair][:]
+            )
+
+        def x_turn(s, b, engine):
+            bank = turn_bank(b % 2)
+            words = x_raw[s, b][:].bitcast(F32)
+            for g in range(NX):
+                for u in range(2):
+                    nc.tensor.transpose(
+                        bank[:, 256 * g + P * u : 256 * g + P * u + P],
+                        words[:, 256 * g + u : 256 * g + 256 : 2],
+                        ident[:],
+                    )
+            dst = x_grp[s, b][:].bitcast(F32).rearrange("p (g r u) -> p g r u", g=2, u=2)
+            frm = bank[:].rearrange("p (g u r) -> p g r u", g=2, u=2)
+            if engine == "scalar":
+                nc.scalar.copy(out=dst, in_=frm)
+            else:
+                nc.vector.tensor_copy(out=dst, in_=frm)
+
+        def x_quant(s, b):
+            nc.vector.quantize_mx(
+                out=x_codes[s, b][:].bitcast(E4M3X4), scales=x_scales[s, b][:], in_=x_grp[s, b][:]
+            )
+
+        wide = {}
+        w_grp = {}
+
+        def w_widen(j, g, n_scalar):
+            wide[j, g] = work.tile([P, 4, N], BF16, tag="wide", name="wide", align_bytes=64)
+            raw, c0 = w_raw[j, g]
+            for t in range(4):
+                src = raw[:, t, c0 : c0 + N].bitcast(E4M3)
+                if t < n_scalar:
+                    nc.scalar.activation(out=wide[j, g][:, t, :], in_=src, func=COPY, scale=w_sc[:, g, t : t + 1])
+                else:
+                    nc.vector.tensor_scalar(
+                        out=wide[j, g][:, t, :], in0=src, scalar1=w_sc[:, g, t : t + 1], scalar2=None, op0=MULT
+                    )
+
+        def w_weave(j, g):
+            w_grp[j, g] = work.tile([P, 4 * N], BF16, tag="w_grp", name="w_grp", align_bytes=64)
+            nc.vector.tensor_copy(
+                out=w_grp[j, g][:].rearrange("p (c i t) -> p c t i", i=4, t=4),
+                in_=wide[j, g][:].rearrange("p t (c i) -> p c t i", i=4),
+            )
+
+        def w_quant(j, g):
+            nc.vector.quantize_mx(
+                out=w_codes[j, g][:].bitcast(E4M3X4), scales=w_planes[j, g][:], in_=w_grp[j, g][:]
+            )
+
+        acc = {}
+
+        def open_group(s, j, b, i):
+            acc[s, j, b] = psum.tile([P, N], F32, tag="acc%d" % i, name="acc%d" % i)
+
+        def u_pass(s, j, b, g, start, stop):
+            pair, half = b // 2, P * (b % 2)
+            nc.tensor.matmul_mx(
+                out=acc[s, j, b][:],
+                lhsT=r_codes[s, g, pair][:, half : half + P].bitcast(E4M3X4),
+                lhsT_scale=r_scales[s, g, pair][:, half : half + P],
+                rhs=u_sb[g][:, 2 * N * j : 2 * N * j + 2 * N].bitcast(E2M1X4),
+                rhs_scale=u_planes[:, g, N * j : N * j + N],
+                start=start,
+                stop=stop,
+            )
+
+        def w_pass(s, j, b, g, start, stop):
+            nc.tensor.matmul_mx(
+                out=acc[s, j, b][:],
+                lhsT=x_codes[s, b][:, P * g : P * g + P].bitcast(E4M3X4),
+                lhsT_scale=x_scales[s, b][:, P * g : P * g + P],
+                rhs=w_codes[j, g][:].bitcast(E4M3X4),
+                rhs_scale=w_planes[j, g][:],
+                start=start,
+                stop=stop,
+            )
+
+        h_sb = {}
+        scaled = {}
+
+        def finish(s, j, b):
+            h = outs.tile([P, N], F32, tag="h", name="h")
+            h_sb[s, j, b] = h
+            nc.scalar.activation(out=h[:], in_=acc[s, j, b][:], func=TANH)
+            out = out_0 if s == 1 else out_1
+            nc.sync.dma_start(out=out[P * b : P * b + P, N * j : N * j + N], in_=h[:])
+
+        def h1_scale(j, b):
+            t = work.tile([P, N], BF16, tag="scaled", name="scaled", bufs=4)
+            scaled[j, b] = t
+            nc.vector.tensor_tensor(
+                out=t[:].rearrange("p (u w e) -> p u w e", u=2, e=2),
+                in0=h_sb[1, j, b][:].rearrange("p (w u e) -> p u w e", u=2, e=2),
+                in1=gain_row[:, N * j : N * j + N].rearrange("p (w u e) -> p u w e", u=2, e=2),
+                op=MULT,
+            )
+
+        def h1_turn(j, pair):
+            bank = turn_bank(pair)
+            for b in range(2):
+                words = scaled[j, 2 * pair + b][:].bitcast(F32)
+                for u in range(2):
+                    nc.tensor.transpose(
+                        bank[:, 256 * u + P * b : 256 * u + P * b + P], words[:, P * u : P * u + P], ident[:]
+                    )
+            nc.scalar.copy(
+                out=r_grp[2, j, pair][:].bitcast(F32).rearrange("p (b u) -> p b u", u=2),
+                in_=bank[:].rearrange("p (u b) -> p b u", u=2),
+            )
+
+        for pair in range(2):
+            h0_turn(0, pair)
+            r_quant(1, 0, pair)
+        first = [(0, 0), (0, 1), (1, 0), (1, 1), (0, 2), (0, 3)]
+        for i, (j, b) in enumerate(first):
+            open_group(1, j, b, i)
+        for j, b in first[:4]:
+            u_pass(1, j, b, 0, True, False)
+        w_widen(0, 0, 4)
+        for pair in range(2):
+            h0_turn(1, pair)
+            r_quant(1, 1, pair)
+        for j, b in first[4:]:
+            u_pass(1, j, b, 0, True, False)
+        w_weave(0, 0)
+        for pair in range(2):
+            h0_turn(2, pair)
+        for j, b in first:
+            u_pass(1, j, b, 1, False, False)
+        for pair in range(2):
+            r_quant(1, 2, pair)
+        w_quant(0, 0)
+        w_widen(0, 1, 3)
+        x_turn(1, 0, "scalar")
+        x_turn(1, 1, "scalar")
+        w_weave(0, 1)
+        for j, b in first:
+            u_pass(1, j, b, 2, False, False)
+        x_quant(1, 0)
+        w_quant(0, 1)
+        x_quant(1, 1)
+        x_turn(1, 2, "scalar")
+        x_turn(1, 3, "vector")
+        x_turn(2, 0, "scalar")
+        x_quant(1, 2)
+        x_turn(2, 1, "vector")
+        x_quant(1, 3)
+        x_turn(2, 2, "scalar")
+        x_quant(2, 0)
+        x_turn(2, 3, "vector")
+        w_widen(1, 0, 3)
+        for b in range(NB):
+            w_pass(1, 0, b, 0, False, False)
+            w_pass(1, 0, b, 1, False, True)
+        finish(1, 0, 0)
+        finish(1, 0, 1)
+        x_quant(2, 1)
+        x_quant(2, 2)
+        w_weave(1, 0)
+        x_quant(2, 3)
+        w_widen(1, 1, 3)
+        w_quant(1, 0)
+        finish(1, 0, 2)
+        finish(1, 0, 3)
+        for i, (j, b) in zip([0, 1, 4, 5], [(1, 2), (1, 3), (2, 0), (2, 1)]):
+            open_group(1, j, b, i)
+            for g in range(NJ):
+                u_pass(1, j, b, g, g == 0, False)
+        w_weave(1, 1)
+        h1_scale(0, 0)
+        w_quant(1, 1)
+        h1_scale(0, 1)
+        w_widen(2, 0, 3)
+        for b in range(NB):
+            w_pass(1, 1, b, 0, False, False)
+            w_pass(1, 1, b, 1, False, True)
+        w_widen(2, 1, 3)
+        w_weave(2, 0)
+        finish(1, 1, 0)
+        finish(1, 1, 1)
+        h1_scale(0, 2)
+        w_quant(2, 0)
+        h1_scale(0, 3)
+        finish(1, 1, 2)
+        finish(1, 1, 3)
+        for i, (j, b) in zip([2, 3], [(2, 2), (2, 3)]):
+            open_group(1, j, b, i)
+            for g in range(NJ):
+                u_pass(1, j, b, g, g == 0, False)
+        for pair in range(2):
+            h1_turn(0, pair)
+        w_weave(2, 1)
+        for pair in range(2):
+            r_quant(2, 0, pair)
+        w_quant(2, 1)
+        for b in range(NB):
+            w_pass(1, 2, b, 0, False, False)
+            w_pass(1, 2, b, 1, False, True)
+        for b in range(NB):
+            finish(1, 2, b)
+        for b in range(NB):
+            h1_scale(1, b)
+        for pair in range(2):
+            h1_turn(1, pair)
+        for b in range(NB):
+            h1_scale(2, b)
+            if b % 2:
+                r_quant(2, 1, b // 2)
+
+        lead = [(0, 0), (0, 1), (0, 2), (0, 3), (1, 0), (1, 1)]
+        lead_banks = [0, 1, 4, 5, 2, 3]
+        for k in range(3):
+            pair_groups = lead[2 * k : 2 * k + 2]
+            for i, (j, b) in enumerate(pair_groups):
+                open_group(2, j, b, lead_banks[2 * k + i])
+                w_pass(2, j, b, 0, True, False)
+                w_pass(2, j, b, 1, False, False)
+                u_pass(2, j, b, 0, False, False)
+            for j, b in pair_groups:
+                u_pass(2, j, b, 1, False, False)
+            if k < 2:
+                h1_turn(2, k)
+                r_quant(2, 2, k)
+        for j, b in lead:
+            u_pass(2, j, b, 2, False, True)
+            finish(2, j, b)
+        for i, (j, b) in enumerate([(1, 2), (1, 3), (2, 0), (2, 1), (2, 2), (2, 3)]):
+            open_group(2, j, b, lead_banks[i])
+            w_pass(2, j, b, 0, True, False)
+            w_pass(2, j, b, 1, False, False)
+            for g in range(NJ):
+                u_pass(2, j, b, g, False, g == NJ - 1)
+            finish(2, j, b)

@@ -32,7 +32,6 @@ def tile_two_step_rnn_fp4_s3_kernel(tc, x1, x2, h0, gain, w_bytes, w_scale, u_wo
         work = ctx.enter_context(tc.tile_pool(name="work", bufs=3))
         outs = ctx.enter_context(tc.tile_pool(name="outs", bufs=12))
         psum = ctx.enter_context(tc.psum_pool(name="psum", bufs=1))
-        ctx.enter_context(tc.manual_schedule())
 
         def keep_tile(shape, dtype, name):
             return keep.tile(shape, dtype, name=name, align_bytes=64)
@@ -55,14 +54,10 @@ def tile_two_step_rnn_fp4_s3_kernel(tc, x1, x2, h0, gain, w_bytes, w_scale, u_wo
         w_raw = {}
         x_raw = {}
 
-        def load_h0(g):
-            for pair in range(2):
-                t = keep_tile([P, 2, N], BF16, "h0_%d_%d" % (g, pair))
-                nc.sync.dma_start(
-                    out=t[:],
-                    in_=h0[256 * pair : 256 * pair + 256, N * g : N * g + N].rearrange("(b p) k -> p b k", p=P),
-                )
-                h0_raw[g, pair] = t
+        def load_h0(b):
+            t = keep_tile([P, H], BF16, "h0_%d" % b)
+            nc.sync.dma_start(out=t[:], in_=h0[P * b : P * b + P, :])
+            h0_raw[b] = t
 
         def load_u(g):
             t = keep_tile([P, 2 * H], U8, "u_%d" % g)
@@ -85,25 +80,27 @@ def tile_two_step_rnn_fp4_s3_kernel(tc, x1, x2, h0, gain, w_bytes, w_scale, u_wo
             for j in range(j0, j1):
                 w_raw[j, g] = (t, N * (j - j0))
 
-        def load_x(s, x):
-            for b in range(NB):
+        def load_x(s, x, bs):
+            for b in bs:
                 t = keep_tile([P, D], BF16, "x%d_%d" % (s, b))
                 nc.sync.dma_start(out=t[:], in_=x[P * b : P * b + P, :])
                 x_raw[s, b] = t
 
         load_h0(0)
-        load_u(0)
-        load_u_scales()
-        load_w(0, 0, 1)
         load_h0(1)
-        load_u(1)
+        load_u_scales()
+        load_u(0)
+        load_w(0, 0, 1)
         load_h0(2)
-        load_u(2)
+        load_h0(3)
+        load_u(1)
         load_w(1, 0, 1)
-        load_x(1, x1)
-        load_x(2, x2)
+        load_x(1, x1, [0, 1])
+        load_u(2)
         load_w(0, 1, 3)
+        load_x(1, x1, [2, 3])
         load_w(1, 1, 3)
+        load_x(2, x2, [0, 1, 2, 3])
         gain_row = keep_tile([P, H], BF16, "gain_row")
         nc.sync.dma_start(out=gain_row[:], in_=gain.partition_broadcast(P))
 
@@ -130,16 +127,16 @@ def tile_two_step_rnn_fp4_s3_kernel(tc, x1, x2, h0, gain, w_bytes, w_scale, u_wo
                 w_planes[j, g] = keep_tile([P, N], U8, "wp_%d_%d" % (j, g))
 
         def turn_bank(i):
-            return psum.tile([P, N], F32, tag="turn%d" % i, name="turn%d" % i)
+            return psum.tile([P, N], F32, tag="turn", name="turn", bufs=2)
 
         def h0_turn(g, pair):
             bank = turn_bank(pair)
-            words = h0_raw[g, pair][:].rearrange("p b k -> p (b k)").bitcast(F32)
-            for u in range(2):
-                for b in range(2):
+            for b in range(2):
+                words = h0_raw[2 * pair + b][:].bitcast(F32)
+                for u in range(2):
                     nc.tensor.transpose(
                         bank[:, 256 * u + P * b : 256 * u + P * b + P],
-                        words[:, 256 * b + u : 256 * b + 256 : 2],
+                        words[:, 256 * g + u : 256 * g + 256 : 2],
                         ident[:],
                     )
             nc.vector.tensor_tensor(
@@ -180,7 +177,7 @@ def tile_two_step_rnn_fp4_s3_kernel(tc, x1, x2, h0, gain, w_bytes, w_scale, u_wo
         w_grp = {}
 
         def w_widen(j, g, n_scalar):
-            wide[j, g] = work.tile([P, 4, N], BF16, tag="wide", name="wide", align_bytes=64)
+            wide[j, g] = work.tile([P, 4, N], BF16, tag="wide", name="wide", align_bytes=64, bufs=6)
             raw, c0 = w_raw[j, g]
             for t in range(4):
                 src = raw[:, t, c0 : c0 + N].bitcast(E4M3)
@@ -205,8 +202,8 @@ def tile_two_step_rnn_fp4_s3_kernel(tc, x1, x2, h0, gain, w_bytes, w_scale, u_wo
 
         acc = {}
 
-        def open_group(s, j, b, i):
-            acc[s, j, b] = psum.tile([P, N], F32, tag="acc%d" % i, name="acc%d" % i)
+        def open_group(s, j, b):
+            acc[s, j, b] = psum.tile([P, N], F32, tag="acc", name="acc", bufs=6)
 
         def u_pass(s, j, b, g, start, stop):
             pair, half = b // 2, P * (b % 2)
@@ -264,126 +261,110 @@ def tile_two_step_rnn_fp4_s3_kernel(tc, x1, x2, h0, gain, w_bytes, w_scale, u_wo
                 in_=bank[:].rearrange("p (u b) -> p b u", u=2),
             )
 
-        for pair in range(2):
-            h0_turn(0, pair)
-            r_quant(1, 0, pair)
-        first = [(0, 0), (0, 1), (1, 0), (1, 1), (0, 2), (0, 3)]
-        for i, (j, b) in enumerate(first):
-            open_group(1, j, b, i)
-        for j, b in first[:4]:
-            u_pass(1, j, b, 0, True, False)
-        w_widen(0, 0, 4)
-        for pair in range(2):
-            h0_turn(1, pair)
-            r_quant(1, 1, pair)
-        for j, b in first[4:]:
-            u_pass(1, j, b, 0, True, False)
-        w_weave(0, 0)
-        for pair in range(2):
-            h0_turn(2, pair)
-        for j, b in first:
-            u_pass(1, j, b, 1, False, False)
-        for pair in range(2):
-            r_quant(1, 2, pair)
-        w_quant(0, 0)
-        w_widen(0, 1, 3)
-        x_turn(1, 0, "scalar")
-        x_turn(1, 1, "scalar")
-        w_weave(0, 1)
-        for j, b in first:
-            u_pass(1, j, b, 2, False, False)
-        x_quant(1, 0)
-        w_quant(0, 1)
-        x_quant(1, 1)
-        x_turn(1, 2, "scalar")
-        x_turn(1, 3, "vector")
-        x_turn(2, 0, "scalar")
-        x_quant(1, 2)
-        x_turn(2, 1, "vector")
-        x_quant(1, 3)
-        x_turn(2, 2, "scalar")
-        x_quant(2, 0)
-        x_turn(2, 3, "vector")
-        w_widen(1, 0, 3)
-        for b in range(NB):
-            w_pass(1, 0, b, 0, False, False)
-            w_pass(1, 0, b, 1, False, True)
-        finish(1, 0, 0)
-        finish(1, 0, 1)
-        x_quant(2, 1)
-        x_quant(2, 2)
-        w_weave(1, 0)
-        x_quant(2, 3)
-        w_widen(1, 1, 3)
-        w_quant(1, 0)
-        finish(1, 0, 2)
-        finish(1, 0, 3)
-        for i, (j, b) in zip([0, 1, 4, 5], [(1, 2), (1, 3), (2, 0), (2, 1)]):
-            open_group(1, j, b, i)
-            for g in range(NJ):
-                u_pass(1, j, b, g, g == 0, False)
-        w_weave(1, 1)
-        h1_scale(0, 0)
-        w_quant(1, 1)
-        h1_scale(0, 1)
-        w_widen(2, 0, 3)
-        for b in range(NB):
-            w_pass(1, 1, b, 0, False, False)
-            w_pass(1, 1, b, 1, False, True)
-        w_widen(2, 1, 3)
-        w_weave(2, 0)
-        finish(1, 1, 0)
-        finish(1, 1, 1)
-        h1_scale(0, 2)
-        w_quant(2, 0)
-        h1_scale(0, 3)
-        finish(1, 1, 2)
-        finish(1, 1, 3)
-        for i, (j, b) in zip([2, 3], [(2, 2), (2, 3)]):
-            open_group(1, j, b, i)
-            for g in range(NJ):
-                u_pass(1, j, b, g, g == 0, False)
-        for pair in range(2):
-            h1_turn(0, pair)
-        w_weave(2, 1)
-        for pair in range(2):
-            r_quant(2, 0, pair)
-        w_quant(2, 1)
-        for b in range(NB):
-            w_pass(1, 2, b, 0, False, False)
-            w_pass(1, 2, b, 1, False, True)
-        for b in range(NB):
-            finish(1, 2, b)
-        for b in range(NB):
-            h1_scale(1, b)
-        for pair in range(2):
-            h1_turn(1, pair)
-        for b in range(NB):
-            h1_scale(2, b)
-            if b % 2:
-                r_quant(2, 1, b // 2)
+        def w_both(s, j, b, first, last):
+            w_pass(s, j, b, 0, first, False)
+            w_pass(s, j, b, 1, False, last)
 
-        lead = [(0, 0), (0, 1), (0, 2), (0, 3), (1, 0), (1, 1)]
-        lead_banks = [0, 1, 4, 5, 2, 3]
-        for k in range(3):
-            pair_groups = lead[2 * k : 2 * k + 2]
-            for i, (j, b) in enumerate(pair_groups):
-                open_group(2, j, b, lead_banks[2 * k + i])
-                w_pass(2, j, b, 0, True, False)
-                w_pass(2, j, b, 1, False, False)
-                u_pass(2, j, b, 0, False, False)
-            for j, b in pair_groups:
-                u_pass(2, j, b, 1, False, False)
-            if k < 2:
-                h1_turn(2, k)
-                r_quant(2, 2, k)
-        for j, b in lead:
-            u_pass(2, j, b, 2, False, True)
+        for g in range(NJ):
+            h0_turn(g, 0)
+            r_quant(1, g, 0)
+        pair0 = [(j, b) for j in range(NJ) for b in (0, 1)]
+        pair1 = [(j, b) for j in range(NJ) for b in (2, 3)]
+        for j, b in pair0:
+            open_group(1, j, b)
+            u_pass(1, j, b, 0, True, False)
+        w_widen(0, 0, 3)
+        for g in range(NJ):
+            h0_turn(g, 1)
+            r_quant(1, g, 1)
+        w_weave(0, 0)
+        w_quant(0, 0)
+        for j, b in pair0:
+            u_pass(1, j, b, 1, False, False)
+        w_widen(0, 1, 3)
+        for b in (0, 1):
+            x_turn(1, b, "scalar")
+            x_quant(1, b)
+        w_weave(0, 1)
+        w_quant(0, 1)
+        for j, b in pair0:
+            u_pass(1, j, b, 2, False, False)
+        for b in (2, 3):
+            x_turn(1, b, "scalar")
+            x_quant(1, b)
+        w_widen(1, 0, 3)
+        w_weave(1, 0)
+        w_quant(1, 0)
+        for b in (0, 1):
+            w_both(1, 0, b, False, True)
+            finish(1, 0, b)
+        w_widen(1, 1, 3)
+        w_weave(1, 1)
+        w_quant(1, 1)
+        for b in (0, 1):
+            x_turn(2, b, "vector")
+            x_quant(2, b)
+        for b in (2, 3):
+            open_group(1, 0, b)
+            for g in range(NJ):
+                u_pass(1, 0, b, g, g == 0, False)
+            w_both(1, 0, b, False, True)
+            finish(1, 0, b)
+        for b in (0, 1):
+            w_both(1, 1, b, False, True)
+            finish(1, 1, b)
+        w_widen(2, 0, 3)
+        w_weave(2, 0)
+        w_quant(2, 0)
+        w_widen(2, 1, 3)
+        w_weave(2, 1)
+        w_quant(2, 1)
+        for b in (2, 3):
+            x_turn(2, b, "scalar")
+            x_quant(2, b)
+        for b in (2, 3):
+            open_group(1, 1, b)
+            for g in range(NJ):
+                u_pass(1, 1, b, g, g == 0, False)
+            w_both(1, 1, b, False, True)
+            finish(1, 1, b)
+
+        def h1_stage(j, pair):
+            for b in (2 * pair, 2 * pair + 1):
+                h1_scale(j, b)
+            h1_turn(j, pair)
+            r_quant(2, j, pair)
+
+        h1_stage(0, 0)
+        for b in (0, 1):
+            open_group(2, 0, b)
+            w_both(2, 0, b, True, False)
+        for b in (2, 3):
+            open_group(1, 2, b)
+            for g in range(NJ):
+                u_pass(1, 2, b, g, g == 0, False)
+        for b in (0, 1, 2, 3):
+            w_both(1, 2, b, False, True)
+            finish(1, 2, b)
+        h1_stage(1, 0)
+        h1_stage(2, 0)
+        h1_stage(0, 1)
+        h1_stage(1, 1)
+        h1_stage(2, 1)
+
+        for b in (0, 1):
+            open_group(2, 1, b)
+            w_both(2, 1, b, True, False)
+            open_group(2, 2, b)
+            w_both(2, 2, b, True, False)
+        for g in range(NJ):
+            for j, b in pair0:
+                u_pass(2, j, b, g, False, g == NJ - 1)
+        for j, b in pair0:
             finish(2, j, b)
-        for i, (j, b) in enumerate([(1, 2), (1, 3), (2, 0), (2, 1), (2, 2), (2, 3)]):
-            open_group(2, j, b, lead_banks[i])
-            w_pass(2, j, b, 0, True, False)
-            w_pass(2, j, b, 1, False, False)
+        for j, b in pair1:
+            open_group(2, j, b)
+            w_both(2, j, b, True, False)
             for g in range(NJ):
                 u_pass(2, j, b, g, False, g == NJ - 1)
             finish(2, j, b)

from contextlib import ExitStack

import concourse.mybir as mybir
from concourse.masks import make_identity

B, D, H = 512, 1024, 1536
FLOPS = 2 * 2 * B * H * (D + H)

F32 = mybir.dt.float32
BF16 = mybir.dt.bfloat16
I32 = mybir.dt.int32
U32 = mybir.dt.uint32
U8 = mybir.dt.uint8
E4M3 = mybir.dt.float8_e4m3fn
E4M3X4 = mybir.dt.float8_e4m3fn_x4
E2M1X4 = mybir.dt.float4_e2m1fn_x4
MULT = mybir.AluOpType.mult
COPY = mybir.ActivationFunctionType.Copy
TANH = mybir.ActivationFunctionType.Tanh

P = 128
N = 512
NB = B // P
NJ = H // N
NX = D // N


def tile_two_step_rnn_fp4_s3_kernel(tc, x1, x2, h0, gain, w_bytes, w_scale, u_words, u_scales, out_0, out_1):
    nc = tc.nc
    with ExitStack() as ctx:
        keep = ctx.enter_context(tc.tile_pool(name="keep", bufs=1))
        work = ctx.enter_context(tc.tile_pool(name="work", bufs=3))
        outs = ctx.enter_context(tc.tile_pool(name="outs", bufs=12))
        psum = ctx.enter_context(tc.psum_pool(name="psum", bufs=1))

        def keep_tile(shape, dtype, name):
            return keep.tile(shape, dtype, name=name, align_bytes=64)

        warm = keep_tile([P, 16], F32, "warm")
        nc.vector.memset(warm[:], 0.0)
        nc.scalar.activation(out=warm[:, 0:1], in_=warm[:, 8:9], func=TANH)
        ident = keep_tile([P, P], F32, "ident")
        make_identity(nc, ident[:])
        u_planes = keep_tile([P, NJ, H], U8, "u_planes")
        nc.vector.memset(u_planes[:].rearrange("p g n -> p (g n)").bitcast(I32), 0)

        gain_col = keep_tile([P, NJ, 4], BF16, "gain_col")
        nc.scalar.dma_start(out=gain_col[:], in_=gain.rearrange("(g p t) -> p g t", p=P, t=4))
        w_sc = keep_tile([P, NX, 4], F32, "w_sc")
        nc.scalar.dma_start(out=w_sc[:], in_=w_scale.rearrange("(g p t) o -> p g (t o)", p=P, t=4))

        h0_raw = {}
        u_sb = {}
        w_raw = {}
        x_raw = {}

        def load_h0(b):
            t = keep_tile([P, H], BF16, "h0_%d" % b)
            nc.sync.dma_start(out=t[:], in_=h0[P * b : P * b + P, :])
            h0_raw[b] = t

        def load_u(g):
            t = keep_tile([P, 2 * H], U8, "u_%d" % g)
            nc.sync.dma_start(out=t[:].bitcast(I32), in_=u_words[g].bitcast(I32))
            u_sb[g] = t

        def load_u_scales():
            for q in range(4):
                nc.sync.dma_start(
                    out=u_planes[32 * q : 32 * q + 4, :, :].bitcast(I32),
                    in_=u_scales[:, 4 * q : 4 * q + 4, :].rearrange("g q n -> q g n").bitcast(I32),
                )

        def load_w(g, j0, j1):
            t = keep_tile([P, 4, N * (j1 - j0)], U8, "w_bytes_%d_%d" % (g, j0))
            nc.sync.dma_start(
                out=t[:],
                in_=w_bytes[N * g : N * g + N, N * j0 : N * j1].rearrange("(p t) n -> p t n", t=4),
            )
            for j in range(j0, j1):
                w_raw[j, g] = (t, N * (j - j0))

        def load_x(s, x, bs):
            for b in bs:
                t = keep_tile([P, D], BF16, "x%d_%d" % (s, b))
                nc.sync.dma_start(out=t[:], in_=x[P * b : P * b + P, :])
                x_raw[s, b] = t

        load_h0(0)
        load_h0(1)
        load_u_scales()
        load_u(0)
        load_w(0, 0, 1)
        load_h0(2)
        load_h0(3)
        load_u(1)
        load_w(1, 0, 1)
        load_x(1, x1, [0, 1])
        load_u(2)
        load_w(0, 1, 3)
        load_x(1, x1, [2, 3])
        load_w(1, 1, 3)
        load_x(2, x2, [0, 1, 2, 3])
        gain_row = keep_tile([P, H], BF16, "gain_row")
        nc.sync.dma_start(out=gain_row[:], in_=gain.partition_broadcast(P))

        r_grp, r_codes, r_scales = {}, {}, {}
        for s in (1, 2):
            for g in range(NJ):
                for pair in range(2):
                    key = "%d_%d_%d" % (s, g, pair)
                    r_grp[s, g, pair] = keep_tile([P, 1024], BF16, "rg_" + key)
                    r_codes[s, g, pair] = keep_tile([P, 256], U32, "rc_" + key)
                    r_scales[s, g, pair] = keep_tile([P, 256], U8, "rs_" + key)
        x_grp, x_codes, x_scales = {}, {}, {}
        for s in (1, 2):
            for b in range(NB):
                key = "%d_%d" % (s, b)
                x_grp[s, b] = keep_tile([P, 1024], BF16, "xg_" + key)
                x_codes[s, b] = keep_tile([P, 256], U32, "xc_" + key)
                x_scales[s, b] = keep_tile([P, 256], U8, "xs_" + key)
        w_codes = {}
        w_planes = {}
        for j in range(NJ):
            for g in range(NX):
                w_codes[j, g] = keep_tile([P, N], U32, "wc_%d_%d" % (j, g))
                w_planes[j, g] = keep_tile([P, N], U8, "wp_%d_%d" % (j, g))

        def turn_bank(i):
            return psum.tile([P, N], F32, tag="turn", name="turn", bufs=2)

        def h0_turn(g, pair):
            bank = turn_bank(pair)
            for b in range(2):
                words = h0_raw[2 * pair + b][:].bitcast(F32)
                for u in range(2):
                    nc.tensor.transpose(
                        bank[:, 256 * u + P * b : 256 * u + P * b + P],
                        words[:, 256 * g + u : 256 * g + 256 : 2],
                        ident[:],
                    )
            nc.vector.tensor_tensor(
                out=r_grp[1, g, pair][:].rearrange("p (b u e) -> p b u e", u=2, e=2),
                in0=bank[:].bitcast(BF16).rearrange("p (u b e) -> p b u e", u=2, e=2),
                in1=gain_col[:, g, :].rearrange("p (u e) -> p u e", e=2).unsqueeze(1).to_broadcast([P, 256, 2, 2]),
                op=MULT,
            )

        def r_quant(s, g, pair):
            nc.vector.quantize_mx(
                out=r_codes[s, g, pair][:].bitcast(E4M3X4), scales=r_scales[s, g, pair][:], in_=r_grp[s, g, pair][:]
            )

        def x_turn(s, b, engine):
            bank = turn_bank(b % 2)
            words = x_raw[s, b][:].bitcast(F32)
            for g in range(NX):
                for u in range(2):
                    nc.tensor.transpose(
                        bank[:, 256 * g + P * u : 256 * g + P * u + P],
                        words[:, 256 * g + u : 256 * g + 256 : 2],
                        ident[:],
                    )
            dst = x_grp[s, b][:].bitcast(F32).rearrange("p (g r u) -> p g r u", g=2, u=2)
            frm = bank[:].rearrange("p (g u r) -> p g r u", g=2, u=2)
            if engine == "scalar":
                nc.scalar.copy(out=dst, in_=frm)
            else:
                nc.vector.tensor_copy(out=dst, in_=frm)

        def x_quant(s, b):
            nc.vector.quantize_mx(
                out=x_codes[s, b][:].bitcast(E4M3X4), scales=x_scales[s, b][:], in_=x_grp[s, b][:]
            )

        wide = {}
        w_grp = {}

        def w_widen(j, g, n_scalar):
            wide[j, g] = work.tile([P, 4, N], BF16, tag="wide", name="wide", align_bytes=64, bufs=6)
            raw, c0 = w_raw[j, g]
            for t in range(4):
                src = raw[:, t, c0 : c0 + N].bitcast(E4M3)
                if t < n_scalar:
                    nc.scalar.activation(out=wide[j, g][:, t, :], in_=src, func=COPY, scale=w_sc[:, g, t : t + 1])
                else:
                    nc.vector.tensor_scalar(
                        out=wide[j, g][:, t, :], in0=src, scalar1=w_sc[:, g, t : t + 1], scalar2=None, op0=MULT
                    )

        def w_weave(j, g):
            w_grp[j, g] = work.tile([P, 4 * N], BF16, tag="w_grp", name="w_grp", align_bytes=64)
            nc.vector.tensor_copy(
                out=w_grp[j, g][:].rearrange("p (c i t) -> p c t i", i=4, t=4),
                in_=wide[j, g][:].rearrange("p t (c i) -> p c t i", i=4),
            )

        def w_quant(j, g):
            nc.vector.quantize_mx(
                out=w_codes[j, g][:].bitcast(E4M3X4), scales=w_planes[j, g][:], in_=w_grp[j, g][:]
            )

        acc = {}

        def open_group(s, j, b):
            acc[s, j, b] = psum.tile([P, N], F32, tag="acc", name="acc", bufs=6)

        def u_pass(s, j, b, g, start, stop):
            pair, half = b // 2, P * (b % 2)
            nc.tensor.matmul_mx(
                out=acc[s, j, b][:],
                lhsT=r_codes[s, g, pair][:, half : half + P].bitcast(E4M3X4),
                lhsT_scale=r_scales[s, g, pair][:, half : half + P],
                rhs=u_sb[g][:, 2 * N * j : 2 * N * j + 2 * N].bitcast(E2M1X4),
                rhs_scale=u_planes[:, g, N * j : N * j + N],
                start=start,
                stop=stop,
            )

        def w_pass(s, j, b, g, start, stop):
            nc.tensor.matmul_mx(
                out=acc[s, j, b][:],
                lhsT=x_codes[s, b][:, P * g : P * g + P].bitcast(E4M3X4),
                lhsT_scale=x_scales[s, b][:, P * g : P * g + P],
                rhs=w_codes[j, g][:].bitcast(E4M3X4),
                rhs_scale=w_planes[j, g][:],
                start=start,
                stop=stop,
            )

        h_sb = {}
        scaled = {}

        def finish(s, j, b):
            h = outs.tile([P, N], F32, tag="h", name="h")
            h_sb[s, j, b] = h
            nc.scalar.activation(out=h[:], in_=acc[s, j, b][:], func=TANH)
            out = out_0 if s == 1 else out_1
            nc.sync.dma_start(out=out[P * b : P * b + P, N * j : N * j + N], in_=h[:])

        def h1_scale(j, b):
            t = work.tile([P, N], BF16, tag="scaled", name="scaled", bufs=4)
            scaled[j, b] = t
            nc.vector.tensor_tensor(
                out=t[:].rearrange("p (u w e) -> p u w e", u=2, e=2),
                in0=h_sb[1, j, b][:].rearrange("p (w u e) -> p u w e", u=2, e=2),
                in1=gain_row[:, N * j : N * j + N].rearrange("p (w u e) -> p u w e", u=2, e=2),
                op=MULT,
            )

        def h1_turn(j, pair):
            bank = turn_bank(pair)
            for b in range(2):
                words = scaled[j, 2 * pair + b][:].bitcast(F32)
                for u in range(2):
                    nc.tensor.transpose(
                        bank[:, 256 * u + P * b : 256 * u + P * b + P], words[:, P * u : P * u + P], ident[:]
                    )
            nc.scalar.copy(
                out=r_grp[2, j, pair][:].bitcast(F32).rearrange("p (b u) -> p b u", u=2),
                in_=bank[:].rearrange("p (u b) -> p b u", u=2),
            )

        def w_both(s, j, b, first, last):
            w_pass(s, j, b, 0, first, False)
            w_pass(s, j, b, 1, False, last)

        for g in range(NJ):
            h0_turn(g, 0)
            r_quant(1, g, 0)
        pair0 = [(j, b) for j in range(NJ) for b in (0, 1)]
        pair1 = [(j, b) for j in range(NJ) for b in (2, 3)]
        for j, b in pair0:
            open_group(1, j, b)
            u_pass(1, j, b, 0, True, False)
        w_widen(0, 0, 3)
        for g in range(NJ):
            h0_turn(g, 1)
            r_quant(1, g, 1)
        w_weave(0, 0)
        w_quant(0, 0)
        for j, b in pair0:
            u_pass(1, j, b, 1, False, False)
        w_widen(0, 1, 3)
        for b in (0, 1):
            x_turn(1, b, "scalar")
            x_quant(1, b)
        w_weave(0, 1)
        w_quant(0, 1)
        for j, b in pair0:
            u_pass(1, j, b, 2, False, False)
        for b in (2, 3):
            x_turn(1, b, "scalar")
            x_quant(1, b)
        w_widen(1, 0, 3)
        w_weave(1, 0)
        w_quant(1, 0)
        for b in (0, 1):
            w_both(1, 0, b, False, True)
            finish(1, 0, b)
        w_widen(1, 1, 3)
        w_weave(1, 1)
        w_quant(1, 1)
        for b in (0, 1):
            x_turn(2, b, "vector")
            x_quant(2, b)
        for b in (2, 3):
            open_group(1, 0, b)
            for g in range(NJ):
                u_pass(1, 0, b, g, g == 0, False)
            w_both(1, 0, b, False, True)
            finish(1, 0, b)
        for b in (0, 1):
            w_both(1, 1, b, False, True)
            finish(1, 1, b)
        w_widen(2, 0, 3)
        w_weave(2, 0)
        w_quant(2, 0)
        w_widen(2, 1, 3)
        w_weave(2, 1)
        w_quant(2, 1)
        for b in (2, 3):
            x_turn(2, b, "scalar")
            x_quant(2, b)
        for b in (2, 3):
            open_group(1, 1, b)
            for g in range(NJ):
                u_pass(1, 1, b, g, g == 0, False)
            w_both(1, 1, b, False, True)
            finish(1, 1, b)

        def h1_stage(j, pair):
            for b in (2 * pair, 2 * pair + 1):
                h1_scale(j, b)
            h1_turn(j, pair)
            r_quant(2, j, pair)

        h1_stage(0, 0)
        for b in (0, 1):
            open_group(2, 0, b)
            w_both(2, 0, b, True, False)
        for b in (2, 3):
            open_group(1, 2, b)
            for g in range(NJ):
                u_pass(1, 2, b, g, g == 0, False)
        for b in (0, 1, 2, 3):
            w_both(1, 2, b, False, True)
            finish(1, 2, b)
        h1_stage(1, 0)
        h1_stage(2, 0)
        h1_stage(0, 1)
        h1_stage(1, 1)
        h1_stage(2, 1)

        for b in (0, 1):
            open_group(2, 1, b)
            w_both(2, 1, b, True, False)
            open_group(2, 2, b)
            w_both(2, 2, b, True, False)
        for g in range(NJ):
            for j, b in pair0:
                u_pass(2, j, b, g, False, g == NJ - 1)
        for j, b in pair0:
            finish(2, j, b)
        for j, b in pair1:
            open_group(2, j, b)
            w_both(2, j, b, True, False)
            for g in range(NJ):
                u_pass(2, j, b, g, False, g == NJ - 1)
            finish(2, j, b)
